import numpy as np
import ml_dtypes


def mxq(x, axis, fmt="e4m3"):
    dtype, down = {"e4m3": (ml_dtypes.float8_e4m3fn, 7), "e5m2": (ml_dtypes.float8_e5m2, 14)}[fmt]
    v = np.moveaxis(np.asarray(x, np.float32).astype(ml_dtypes.bfloat16).astype(np.float64), axis, -1)
    blocks = v.reshape(v.shape[:-1] + (-1, 32))
    amax = np.abs(blocks).max(-1, keepdims=True)
    byte = np.maximum(np.where(amax > 0, np.frexp(amax)[1] - 1 + 127, 0) - down, 1)
    scale = np.exp2(byte - 127.0)
    codes = (blocks / scale).astype(np.float32).astype(dtype).astype(np.float64)
    return np.moveaxis((codes * scale).reshape(v.shape), -1, axis)


WIDE = False


def mx_kscale(k):
    if not WIDE:
        return np.ones(k)
    levels = np.array([30, -30])
    if k % 512:
        return np.exp2(np.random.permutation(np.resize(levels, k // 32))).repeat(32)
    a = np.empty((k // 512, 16))
    for p in range(k // 512):
        a[p, :8] = np.random.permutation(np.resize(levels, 8))
        for g in range(8):
            far = levels[np.abs(levels - a[p, g]) >= 10]
            a[p, g + 8] = far[np.random.randint(len(far))]
    return np.exp2(a.ravel()).repeat(32)


def f64(x):
    return np.asarray(x).astype(np.float64)


def striped(idx):
    return np.tile(np.asarray(idx).reshape(-1, 16).T, (8, 1)).astype(np.uint16)


def unstriped(offs):
    return offs[:16].T.reshape(-1).astype(np.int64)


E2M1 = np.array([0.0, 0.5, 1.0, 1.5, 2.0, 3.0, 4.0, 6.0, -0.0, -0.5, -1.0, -1.5, -2.0, -3.0, -4.0, -6.0])


def pack_weight(w, fmt):
    k, n = w.shape
    w = f64(np.asarray(w, np.float32).astype(ml_dtypes.bfloat16)).reshape(k // 32, 32, n)
    amax = np.abs(w).max(1)
    if fmt == "e4m3":
        byte = np.frexp(amax)[1] - 1 + 127 - 7
    else:
        mant, ex = np.frexp(amax / 6.0)
        byte = np.where(mant > 0.5, ex, ex - 1) + 127
    byte = np.clip(np.where(amax > 0, byte, 1), 1, 254)
    scaled = (w * np.exp2(127.0 - byte)[:, None, :]).reshape(k, n).astype(np.float32)
    by_word = np.ascontiguousarray(scaled.reshape(k // 512, 128, 4, n).transpose(0, 1, 3, 2))
    if fmt == "e4m3":
        words = by_word.astype(ml_dtypes.float8_e4m3fn).view(np.uint8)
    else:
        c = by_word.astype(ml_dtypes.float4_e2m1fn).view(np.uint8) & 0xF
        words = (c[..., 0::2] | (c[..., 1::2] << 4)).reshape(k // 512, 128, 2 * n)
    return np.ascontiguousarray(words), np.ascontiguousarray(byte.astype(np.uint8).reshape(k // 512, 16, n))


def unpack_weight(words, scales, fmt):
    g, _, n = scales.shape
    words = np.ascontiguousarray(words).reshape(g, 128, n, -1)
    if fmt == "e4m3":
        vals = words.view(ml_dtypes.float8_e4m3fn).astype(np.float64)
    else:
        nib = np.empty((g, 128, n, 4), np.uint8)
        nib[..., 0::2] = words & 0xF
        nib[..., 1::2] = words >> 4
        vals = E2M1[nib]
    vals = vals * np.repeat(np.exp2(scales.astype(np.float64) - 127.0), 8, axis=1)[..., None]
    return vals.transpose(0, 1, 3, 2).reshape(g * 512, n)


K, R, N, T, J = 512, 512, 512, 1024, 512


def setup_inputs():
    n = np.random.standard_normal
    idx = np.random.permutation(T)[:J]
    fj = mx_kscale(J)
    fn = mx_kscale(N)
    tj = np.ones(T)
    tj[idx] = fj
    wdp = pack_weight(n((N, R)) * 1 / np.sqrt(N) * fn[:, None], "e2m1")
    return {
        "xt": (n((K, T)) * tj).astype(np.float32),
        "g": (n((N, T)) * np.exp(0.5 * n((1, T))) / fn[:, None]).astype(np.float32),
        "wd_words": wdp[0],
        "wd_scales": wdp[1],
        "sv": (n((R, T))).astype(np.float32),
        "rw": (np.random.uniform(0.4, 1.2, (1, J)) / fj).astype(np.float32),
        "offs": striped(idx),
    }


def reference(xt, g, wd_words, wd_scales, sv, rw, offs):
    idx = unstriped(offs)
    wdu = unpack_weight(wd_words, wd_scales, "e2m1")
    gidxq = mxq(f64(g)[:, idx], 0, "e5m2")
    d = wdu.T @ gidxq
    dz = d * np.maximum(f64(sv)[:, idx], 0.0) * f64(rw)
    dt1 = dz.T
    xj = f64(xt)[:, idx].T
    xjq = mxq(xj, 0, "e4m3")
    dt1q = mxq(dt1, 0, "e5m2")
    w = xjq.T @ dt1q
    y = 0.04 * w
    return y

@@ -1,0 +1,197 @@
+from contextlib import ExitStack
+
+import concourse.mybir as mybir
+from concourse.masks import make_identity
+
+K, R, N, T, J = 512, 512, 512, 1024, 512
+FLOPS = 2 * N * R * J + 2 * J * K * R
+
+F32 = mybir.dt.float32
+BF16 = mybir.dt.bfloat16
+I32 = mybir.dt.int32
+U32 = mybir.dt.uint32
+U16 = mybir.dt.uint16
+U8 = mybir.dt.uint8
+E4M3 = mybir.dt.float8_e4m3fn_x4
+E5M2 = mybir.dt.float8_e5m2_x4
+E2M1 = mybir.dt.float4_e2m1fn_x4
+COPY = mybir.ActivationFunctionType.Copy
+MULT = mybir.AluOpType.mult
+MAX = mybir.AluOpType.max
+
+P = 128
+PACK = 4
+BLOCKS = 4
+OUT_SCALE = 0.04
+G_LAST_PIECES = 4
+SCALAR_X = (0, 2)
+
+
+def tile_moe_expert_first_layer_wgrad_kernel(tc, xt, g, wd_words, wd_scales, sv, rw, offs, out):
+    nc = tc.nc
+    with ExitStack() as ctx:
+        keep = ctx.enter_context(tc.tile_pool(name="keep", bufs=1))
+        psum = ctx.enter_context(tc.psum_pool(name="psum", bufs=1))
+
+        offsets = keep.tile([P, J // 16], U16, name="offsets")
+        nc.sync.dma_start(offsets[:], offs)
+
+        wd_plane = keep.tile([P, R], U8, name="wd_plane", align_bytes=64)
+        nc.gpsimd.memset(wd_plane[:].bitcast(I32), 0)
+        ident = keep.tile([P, P], F32, name="ident")
+        make_identity(nc, ident[:])
+
+        g_rows = g.rearrange("(p q) t -> p q t", q=PACK)
+        g_in = [keep.tile([P, T], F32, name=f"g_in{q}") for q in range(PACK)]
+        sv_in = [keep.tile([P, T], F32, name=f"sv_in{a}") for a in range(BLOCKS)]
+        x_in = [keep.tile([P, T], F32, name=f"x_in{a}", align_bytes=64) for a in range(BLOCKS)]
+        wd_codes = keep.tile([P, 2 * R], U8, name="wd_codes", align_bytes=64)
+        rw_col = keep.tile([P, PACK], F32, name="rw_col", align_bytes=64)
+        for q in range(PACK):
+            nc.sync.dma_start(g_in[q][:], g_rows[:, q, :])
+            nc.sync.dma_start(
+                wd_plane[:].bitcast(I32)[32 * q : 32 * q + 4, :],
+                wd_scales[0].bitcast(I32)[4 * q : 4 * q + 4, :],
+            )
+
+        def load_rows(tile, src, a):
+            nc.sync.dma_start(tile[a][:], src[a * P : (a + 1) * P, :])
+
+        load_rows(sv_in, sv, 0)
+        nc.sync.dma_start(wd_codes[:].bitcast(I32), wd_words[0].bitcast(I32))
+        load_rows(sv_in, sv, 1)
+        nc.sync.dma_start(rw_col[:], rw.rearrange("o (p t) -> p (o t)", t=PACK))
+        load_rows(x_in, xt, 0)
+        load_rows(sv_in, sv, 2)
+        load_rows(sv_in, sv, 3)
+        for a in range(1, BLOCKS):
+            load_rows(x_in, xt, a)
+
+        g_picked = keep.tile([P, PACK, J], F32, name="g_picked")
+        g_bf = keep.tile([P, PACK, P, PACK], BF16, name="g_bf", align_bytes=64)
+        for q in range(PACK - 1):
+            nc.vector.tensor_copy(g_picked[:, q, :], g_in[q][:].indirect(offsets[:]))
+        piece = J // G_LAST_PIECES
+        for h in range(G_LAST_PIECES):
+            cols = slice(h * piece, (h + 1) * piece)
+            nc.vector.tensor_copy(
+                g_picked[:, PACK - 1, cols],
+                g_in[PACK - 1][:].indirect(offsets[:, h * piece // 16 : (h + 1) * piece // 16]),
+            )
+            nc.scalar.activation(
+                g_bf[:, :, h * piece // PACK : (h + 1) * piece // PACK, :].rearrange("p t m q -> p m q t"),
+                g_picked[:, :, cols].rearrange("p q (m t) -> p m q t", t=PACK),
+                COPY,
+            )
+
+        sv_turned = []
+
+        def turn_sv(a):
+            picked = keep.tile([P, J], F32, name=f"sv_picked{a}")
+            nc.vector.tensor_copy(picked[:], sv_in[a][:].indirect(offsets[:]))
+            bank = psum.tile([P, PACK, P], F32, name=f"sv_turned{a}", tag=f"bank_b{a}")
+            for t in range(PACK):
+                nc.tensor.transpose(bank[:, t, :], picked[:, t::PACK], ident[:])
+            sv_turned.append(bank)
+
+        turn_sv(0)
+        turn_sv(1)
+
+        x_cast = {}
+
+        def cast_x(a):
+            x_cast[a] = keep.tile([P, T], BF16, name=f"x_cast{a}")
+            nc.scalar.activation(x_cast[a][:], x_in[a][:], COPY)
+
+        cast_x(0)
+
+        g_codes = keep.tile([P, J], U32, name="g_codes", align_bytes=64)
+        g_plane = keep.tile([P, J], U8, name="g_plane", align_bytes=64)
+        nc.vector.quantize_mx(g_codes[:].bitcast(E5M2), g_plane[:], g_bf[:].rearrange("p t m q -> p (t m q)"))
+
+        d_rw = keep.tile([P, PACK, R], F32, name="d_rw", tag="x_in0", align_bytes=64)
+        for t in range(PACK):
+            cols = slice(t * P, (t + 1) * P)
+            bank = psum.tile([P, R], F32, name=f"d{t}", tag=f"bank_a{t}")
+            nc.tensor.matmul_mx(
+                bank[:], lhsT=g_codes[:, cols].bitcast(E5M2), lhsT_scale=g_plane[:, cols],
+                rhs=wd_codes[:].bitcast(E2M1), rhs_scale=wd_plane[:], start=True, stop=True,
+            )
+            nc.scalar.activation(d_rw[:, t, :], bank[:], COPY, scale=rw_col[:, t : t + 1])
+
+        turn_sv(2)
+        turn_sv(3)
+
+        x_bf = {}
+
+        def turn_x(a):
+            tag = {0: "rw_col", 3: "dz_bf3"}.get(a, f"x_picked{a}")
+            picked = keep.tile([P, J], BF16, name=f"x_picked{a}", tag=tag, align_bytes=64)
+            if a in SCALAR_X:
+                nc.scalar.activation(picked[:], x_cast[a][:].indirect(offsets[:]), COPY)
+            else:
+                nc.vector.tensor_copy(picked[:], x_in[a][:].indirect(offsets[:]))
+            words = picked[:].bitcast(F32)
+            bank = psum.tile([P, 2, P], F32, name=f"x_turned{a}", tag=f"bank_a{a}")
+            for u in range(2):
+                nc.tensor.transpose(bank[:, u, :], words[:, u::2], ident[:])
+            grouped = keep.tile([P, P * PACK], BF16, name=f"x_bf{a}", align_bytes=64)
+            nc.scalar.copy(
+                grouped[:].bitcast(F32).rearrange("p (k u) -> p k u", u=2),
+                bank[:].rearrange("p u k -> p k u"),
+            )
+            x_bf[a] = grouped
+
+        turn_x(1)
+        turn_x(0)
+        cast_x(2)
+
+        dz_bf = [keep.tile([P, P, PACK], BF16, name=f"dz_bf{a}", tag=("x_in1" if a == 0 else f"dz_bf{a}"), align_bytes=64) for a in range(BLOCKS)]
+        dz_codes = keep.tile([P, R], U32, name="dz_codes", align_bytes=64)
+        dz_plane = keep.tile([P, R], U8, name="dz_plane", align_bytes=64)
+
+        def quantise_dz(a):
+            cols = slice(a * P, (a + 1) * P)
+            nc.vector.quantize_mx(
+                dz_codes[:, cols].bitcast(E5M2), dz_plane[:, cols], dz_bf[a][:].rearrange("p r t -> p (r t)")
+            )
+
+        x_codes, x_plane = {}, {}
+
+        def quantise_x(a):
+            x_codes[a] = keep.tile([P, P], U32, name=f"x_codes{a}", align_bytes=64)
+            x_plane[a] = keep.tile([P, P], U8, name=f"x_plane{a}", align_bytes=64)
+            nc.vector.quantize_mx(x_codes[a][:].bitcast(E4M3), x_plane[a][:], x_bf[a][:])
+
+        for a in range(BLOCKS):
+            nc.vector.scalar_tensor_tensor(
+                dz_bf[a][:], sv_turned[a][:].rearrange("p t r -> p r t"), 0.0,
+                d_rw[:, :, a * P : (a + 1) * P].rearrange("p t r -> p r t"), MAX, MULT,
+            )
+            if a > 0:
+                quantise_dz(a - 1)
+        quantise_x(1)
+        quantise_dz(BLOCKS - 1)
+        quantise_x(0)
+
+        def finish(a):
+            bank = psum.tile([P, R], F32, name=f"w{a}", tag=f"bank_b{a}")
+            nc.tensor.matmul_mx(
+                bank[:], lhsT=x_codes[a][:].bitcast(E4M3), lhsT_scale=x_plane[a][:],
+                rhs=dz_codes[:].bitcast(E5M2), rhs_scale=dz_plane[:], start=True, stop=True,
+            )
+            result = keep.tile([P, R], F32, name=f"result{a}")
+            if a % 2 == 0:
+                nc.scalar.activation(result[:], bank[:], COPY, scale=OUT_SCALE)
+            else:
+                nc.vector.tensor_scalar(result[:], bank[:], OUT_SCALE, None, MULT)
+            nc.sync.dma_start(out[a * P : (a + 1) * P, :], result[:])
+
+        turn_x(3)
+        turn_x(2)
+        finish(1)
+        finish(0)
+        quantise_x(3)
+        quantise_x(2)
+        finish(3)
+        finish(2)

@@ -23,8 +23,8 @@ P = 128
 PACK = 4
 BLOCKS = 4
 OUT_SCALE = 0.04
-G_LAST_PIECES = 4
-SCALAR_X = (0, 2)
+SCALAR_X = (0,)
+X_GROUPS = ((0, 1), (2,), (3,))
 
 
 def tile_moe_expert_first_layer_wgrad_kernel(tc, xt, g, wd_words, wd_scales, sv, rw, offs, out):
@@ -34,10 +34,11 @@ def tile_moe_expert_first_layer_wgrad_kernel(tc, xt, g, wd_words, wd_scales, sv,
         psum = ctx.enter_context(tc.psum_pool(name="psum", bufs=1))
 
         offsets = keep.tile([P, J // 16], U16, name="offsets")
-        nc.sync.dma_start(offsets[:], offs)
 
         wd_plane = keep.tile([P, R], U8, name="wd_plane", align_bytes=64)
         nc.gpsimd.memset(wd_plane[:].bitcast(I32), 0)
+        rw_rows = keep.tile([P, P], F32, name="rw_rows")
+        nc.gpsimd.memset(rw_rows[:], 0.0)
         ident = keep.tile([P, P], F32, name="ident")
         make_identity(nc, ident[:])
 
@@ -46,9 +47,10 @@ def tile_moe_expert_first_layer_wgrad_kernel(tc, xt, g, wd_words, wd_scales, sv,
         sv_in = [keep.tile([P, T], F32, name=f"sv_in{a}") for a in range(BLOCKS)]
         x_in = [keep.tile([P, T], F32, name=f"x_in{a}", align_bytes=64) for a in range(BLOCKS)]
         wd_codes = keep.tile([P, 2 * R], U8, name="wd_codes", align_bytes=64)
-        rw_col = keep.tile([P, PACK], F32, name="rw_col", align_bytes=64)
         for q in range(PACK):
             nc.sync.dma_start(g_in[q][:], g_rows[:, q, :])
+            if q == 0:
+                nc.sync.dma_start(offsets[:], offs)
             nc.sync.dma_start(
                 wd_plane[:].bitcast(I32)[32 * q : 32 * q + 4, :],
                 wd_scales[0].bitcast(I32)[4 * q : 4 * q + 4, :],
@@ -57,141 +59,143 @@ def tile_moe_expert_first_layer_wgrad_kernel(tc, xt, g, wd_words, wd_scales, sv,
         def load_rows(tile, src, a):
             nc.sync.dma_start(tile[a][:], src[a * P : (a + 1) * P, :])
 
+        nc.sync.dma_start(rw_rows[0:BLOCKS, :], rw.rearrange("o (b p) -> (o b) p", p=P))
         load_rows(sv_in, sv, 0)
         nc.sync.dma_start(wd_codes[:].bitcast(I32), wd_words[0].bitcast(I32))
         load_rows(sv_in, sv, 1)
-        nc.sync.dma_start(rw_col[:], rw.rearrange("o (p t) -> p (o t)", t=PACK))
-        load_rows(x_in, xt, 0)
         load_rows(sv_in, sv, 2)
         load_rows(sv_in, sv, 3)
-        for a in range(1, BLOCKS):
+        for a in range(BLOCKS):
             load_rows(x_in, xt, a)
 
+        rw_turned = psum.tile([P, P], F32, name="rw_turned", tag="bank_b0")
+        nc.tensor.transpose(rw_turned[:], rw_rows[:], ident[:])
+        rw_col = keep.tile([P, BLOCKS], F32, name="rw_col", align_bytes=64)
+        nc.scalar.copy(rw_col[:], rw_turned[:, 0:BLOCKS])
+
         g_picked = keep.tile([P, PACK, J], F32, name="g_picked")
-        g_bf = keep.tile([P, PACK, P, PACK], BF16, name="g_bf", align_bytes=64)
+        g_bf = [keep.tile([P, 2 * P, PACK], BF16, name=f"g_bf{h}", align_bytes=64) for h in range(2)]
         for q in range(PACK - 1):
             nc.vector.tensor_copy(g_picked[:, q, :], g_in[q][:].indirect(offsets[:]))
-        piece = J // G_LAST_PIECES
-        for h in range(G_LAST_PIECES):
-            cols = slice(h * piece, (h + 1) * piece)
+        for b in range(BLOCKS):
+            cols = slice(b * P, (b + 1) * P)
             nc.vector.tensor_copy(
                 g_picked[:, PACK - 1, cols],
-                g_in[PACK - 1][:].indirect(offsets[:, h * piece // 16 : (h + 1) * piece // 16]),
+                g_in[PACK - 1][:].indirect(offsets[:, b * P // 16 : (b + 1) * P // 16]),
             )
             nc.scalar.activation(
-                g_bf[:, :, h * piece // PACK : (h + 1) * piece // PACK, :].rearrange("p t m q -> p m q t"),
-                g_picked[:, :, cols].rearrange("p q (m t) -> p m q t", t=PACK),
+                g_bf[b // 2][:, (b % 2) * P : (b % 2 + 1) * P, :].rearrange("p (c i) q -> p c q i", i=4),
+                g_picked[:, :, cols].rearrange("p q (c i) -> p c q i", i=4),
                 COPY,
             )
 
-        sv_turned = []
+        sv_picked = []
 
-        def turn_sv(a):
-            picked = keep.tile([P, J], F32, name=f"sv_picked{a}")
+        def pick_sv(a):
+            tag = "g_bf1" if a == 1 else f"sv_picked{a}"
+            picked = keep.tile([P, J], F32, name=f"sv_picked{a}", tag=tag, align_bytes=64)
             nc.vector.tensor_copy(picked[:], sv_in[a][:].indirect(offsets[:]))
-            bank = psum.tile([P, PACK, P], F32, name=f"sv_turned{a}", tag=f"bank_b{a}")
-            for t in range(PACK):
-                nc.tensor.transpose(bank[:, t, :], picked[:, t::PACK], ident[:])
-            sv_turned.append(bank)
+            sv_picked.append(picked)
 
-        turn_sv(0)
-        turn_sv(1)
+        g_codes = [keep.tile([P, 2 * P], U32, name=f"g_codes{h}", align_bytes=64) for h in range(2)]
+        g_plane = [keep.tile([P, 2 * P], U8, name=f"g_plane{h}", align_bytes=64) for h in range(2)]
+        pick_sv(0)
+        for h in range(2):
+            nc.vector.quantize_mx(g_codes[h][:].bitcast(E5M2), g_plane[h][:], g_bf[h][:].rearrange("p j q -> p (j q)"))
 
-        x_cast = {}
+        x_cast, x_picked = {}, {}
 
         def cast_x(a):
-            x_cast[a] = keep.tile([P, T], BF16, name=f"x_cast{a}")
+            x_cast[a] = keep.tile([P, T], BF16, name=f"x_cast{a}", align_bytes=64)
             nc.scalar.activation(x_cast[a][:], x_in[a][:], COPY)
 
-        cast_x(0)
+        def pick_x(a):
+            tag = {3: "x_bf0"}.get(a, f"x_picked{a}")
+            x_picked[a] = keep.tile([P, J], BF16, name=f"x_picked{a}", tag=tag, align_bytes=64)
+            if a in SCALAR_X:
+                nc.scalar.activation(x_picked[a][:], x_cast[a][:].indirect(offsets[:]), COPY)
+            else:
+                nc.vector.tensor_copy(x_picked[a][:], x_in[a][:].indirect(offsets[:]))
 
-        g_codes = keep.tile([P, J], U32, name="g_codes", align_bytes=64)
-        g_plane = keep.tile([P, J], U8, name="g_plane", align_bytes=64)
-        nc.vector.quantize_mx(g_codes[:].bitcast(E5M2), g_plane[:], g_bf[:].rearrange("p t m q -> p (t m q)"))
-
-        d_rw = keep.tile([P, PACK, R], F32, name="d_rw", tag="x_in0", align_bytes=64)
-        for t in range(PACK):
-            cols = slice(t * P, (t + 1) * P)
-            bank = psum.tile([P, R], F32, name=f"d{t}", tag=f"bank_a{t}")
+        d_rw = keep.tile([P, BLOCKS, R], F32, name="d_rw")
+        d_turned = [psum.tile([P, J], F32, name=f"d_turned{a}", tag=f"bank_b{a}") for a in range(BLOCKS)]
+        for b in range(BLOCKS):
+            cols = slice((b % 2) * P, (b % 2 + 1) * P)
+            bank = psum.tile([P, R], F32, name=f"d{b}", tag=f"bank_a{b}")
             nc.tensor.matmul_mx(
-                bank[:], lhsT=g_codes[:, cols].bitcast(E5M2), lhsT_scale=g_plane[:, cols],
+                bank[:], lhsT=g_codes[b // 2][:, cols].bitcast(E5M2), lhsT_scale=g_plane[b // 2][:, cols],
                 rhs=wd_codes[:].bitcast(E2M1), rhs_scale=wd_plane[:], start=True, stop=True,
             )
-            nc.scalar.activation(d_rw[:, t, :], bank[:], COPY, scale=rw_col[:, t : t + 1])
+            nc.scalar.activation(d_rw[:, b, :], bank[:], COPY, scale=rw_col[:, b : b + 1])
 
-        turn_sv(2)
-        turn_sv(3)
+        for b in range(BLOCKS):
+            for a in range(BLOCKS):
+                nc.tensor.transpose(d_turned[a][:, b * P : (b + 1) * P], d_rw[:, b, a * P : (a + 1) * P], ident[:])
 
-        x_bf = {}
+        for a in range(1, BLOCKS):
+            pick_sv(a)
+        cast_x(0)
+        pick_x(0)
 
-        def turn_x(a):
-            tag = {0: "rw_col", 3: "dz_bf3"}.get(a, f"x_picked{a}")
-            picked = keep.tile([P, J], BF16, name=f"x_picked{a}", tag=tag, align_bytes=64)
-            if a in SCALAR_X:
-                nc.scalar.activation(picked[:], x_cast[a][:].indirect(offsets[:]), COPY)
-            else:
-                nc.vector.tensor_copy(picked[:], x_in[a][:].indirect(offsets[:]))
-            words = picked[:].bitcast(F32)
-            bank = psum.tile([P, 2, P], F32, name=f"x_turned{a}", tag=f"bank_a{a}")
+        x_bf = [keep.tile([P, len(group) * P * PACK], BF16, name=f"x_bf{h}", align_bytes=64) for h, group in enumerate(X_GROUPS)]
+        x_place = {a: (h, i) for h, group in enumerate(X_GROUPS) for i, a in enumerate(group)}
+        dz_bf = keep.tile([P, R * PACK], BF16, name="dz_bf", align_bytes=64)
+
+        def turn(rows, bank_tag, grouped, copy):
+            words = rows[:].bitcast(F32)
+            bank = psum.tile([P, 2, P], F32, name="turned", tag=bank_tag)
             for u in range(2):
                 nc.tensor.transpose(bank[:, u, :], words[:, u::2], ident[:])
-            grouped = keep.tile([P, P * PACK], BF16, name=f"x_bf{a}", align_bytes=64)
-            nc.scalar.copy(
-                grouped[:].bitcast(F32).rearrange("p (k u) -> p k u", u=2),
-                bank[:].rearrange("p u k -> p k u"),
-            )
-            x_bf[a] = grouped
+            copy(grouped.rearrange("p (c u) -> p c u", u=2), bank[:].rearrange("p u c -> p c u"))
 
-        turn_x(1)
-        turn_x(0)
-        cast_x(2)
+        def turn_x(a, bank):
+            h, i = x_place[a]
+            turn(x_picked[a], f"bank_a{bank}", x_bf[h][:].bitcast(F32)[:, i * 2 * P : (i + 1) * 2 * P], nc.vector.tensor_copy if a == BLOCKS - 1 else nc.scalar.copy)
 
-        dz_bf = [keep.tile([P, P, PACK], BF16, name=f"dz_bf{a}", tag=("x_in1" if a == 0 else f"dz_bf{a}"), align_bytes=64) for a in range(BLOCKS)]
         dz_codes = keep.tile([P, R], U32, name="dz_codes", align_bytes=64)
         dz_plane = keep.tile([P, R], U8, name="dz_plane", align_bytes=64)
+        x_codes = [keep.tile([P, len(group) * P], U32, name=f"x_codes{h}", align_bytes=64) for h, group in enumerate(X_GROUPS)]
+        x_plane = [keep.tile([P, len(group) * P], U8, name=f"x_plane{h}", align_bytes=64) for h, group in enumerate(X_GROUPS)]
 
-        def quantise_dz(a):
-            cols = slice(a * P, (a + 1) * P)
-            nc.vector.quantize_mx(
-                dz_codes[:, cols].bitcast(E5M2), dz_plane[:, cols], dz_bf[a][:].rearrange("p r t -> p (r t)")
-            )
+        def make_dz(a):
+            rows = keep.tile([P, J], BF16, name=f"dz_rows{a}", align_bytes=64)
+            nc.vector.scalar_tensor_tensor(rows[:], sv_picked[a][:], 0.0, d_turned[a][:], MAX, MULT)
+            turn(rows, f"bank_a{(a + 2) % 4}", dz_bf[:].bitcast(F32)[:, a * 2 * P : (a + 1) * 2 * P], nc.scalar.copy)
 
-        x_codes, x_plane = {}, {}
-
-        def quantise_x(a):
-            x_codes[a] = keep.tile([P, P], U32, name=f"x_codes{a}", align_bytes=64)
-            x_plane[a] = keep.tile([P, P], U8, name=f"x_plane{a}", align_bytes=64)
-            nc.vector.quantize_mx(x_codes[a][:].bitcast(E4M3), x_plane[a][:], x_bf[a][:])
-
-        for a in range(BLOCKS):
-            nc.vector.scalar_tensor_tensor(
-                dz_bf[a][:], sv_turned[a][:].rearrange("p t r -> p r t"), 0.0,
-                d_rw[:, :, a * P : (a + 1) * P].rearrange("p t r -> p r t"), MAX, MULT,
-            )
-            if a > 0:
-                quantise_dz(a - 1)
-        quantise_x(1)
-        quantise_dz(BLOCKS - 1)
-        quantise_x(0)
+        def quantise_x(h):
+            nc.vector.quantize_mx(x_codes[h][:].bitcast(E4M3), x_plane[h][:], x_bf[h][:])
 
         def finish(a):
+            h, i = x_place[a]
+            cols = slice(i * P, (i + 1) * P)
             bank = psum.tile([P, R], F32, name=f"w{a}", tag=f"bank_b{a}")
             nc.tensor.matmul_mx(
-                bank[:], lhsT=x_codes[a][:].bitcast(E4M3), lhsT_scale=x_plane[a][:],
+                bank[:], lhsT=x_codes[h][:, cols].bitcast(E4M3), lhsT_scale=x_plane[h][:, cols],
                 rhs=dz_codes[:].bitcast(E5M2), rhs_scale=dz_plane[:], start=True, stop=True,
             )
             result = keep.tile([P, R], F32, name=f"result{a}")
-            if a % 2 == 0:
+            if a < BLOCKS - 1:
                 nc.scalar.activation(result[:], bank[:], COPY, scale=OUT_SCALE)
+                nc.sync.dma_start(out[a * P : (a + 1) * P, :], result[:])
             else:
-                nc.vector.tensor_scalar(result[:], bank[:], OUT_SCALE, None, MULT)
-            nc.sync.dma_start(out[a * P : (a + 1) * P, :], result[:])
+                for half in (slice(0, R // 2), slice(R // 2, R)):
+                    nc.vector.tensor_scalar(result[:, half], bank[:, half], OUT_SCALE, None, MULT)
+                    nc.sync.dma_start(out[a * P : (a + 1) * P, half], result[:, half])
 
-        turn_x(3)
-        turn_x(2)
-        finish(1)
+        for a in range(BLOCKS):
+            make_dz(a)
+        turn_x(0, 2)
+        pick_x(1)
+        turn_x(1, 3)
+        pick_x(2)
+        turn_x(2, 0)
+        nc.vector.quantize_mx(dz_codes[:].bitcast(E5M2), dz_plane[:], dz_bf[:])
+        quantise_x(0)
+        pick_x(3)
         finish(0)
-        quantise_x(3)
+        finish(1)
+        turn_x(3, 1)
+        quantise_x(1)
+        finish(2)
         quantise_x(2)
         finish(3)
-        finish(2)

from contextlib import ExitStack

import concourse.mybir as mybir
from concourse.masks import make_identity

K, R, N, T, J = 512, 512, 512, 1024, 512
FLOPS = 2 * N * R * J + 2 * J * K * R

F32 = mybir.dt.float32
BF16 = mybir.dt.bfloat16
I32 = mybir.dt.int32
U32 = mybir.dt.uint32
U16 = mybir.dt.uint16
U8 = mybir.dt.uint8
E4M3 = mybir.dt.float8_e4m3fn_x4
E5M2 = mybir.dt.float8_e5m2_x4
E2M1 = mybir.dt.float4_e2m1fn_x4
COPY = mybir.ActivationFunctionType.Copy
MULT = mybir.AluOpType.mult
MAX = mybir.AluOpType.max

P = 128
PACK = 4
BLOCKS = 4
OUT_SCALE = 0.04
SCALAR_X = (0,)
X_GROUPS = ((0, 1), (2,), (3,))


def tile_moe_expert_first_layer_wgrad_kernel(tc, xt, g, wd_words, wd_scales, sv, rw, offs, out):
    nc = tc.nc
    with ExitStack() as ctx:
        keep = ctx.enter_context(tc.tile_pool(name="keep", bufs=1))
        psum = ctx.enter_context(tc.psum_pool(name="psum", bufs=1))

        offsets = keep.tile([P, J // 16], U16, name="offsets")

        wd_plane = keep.tile([P, R], U8, name="wd_plane", align_bytes=64)
        nc.gpsimd.memset(wd_plane[:].bitcast(I32), 0)
        rw_rows = keep.tile([P, P], F32, name="rw_rows")
        nc.gpsimd.memset(rw_rows[:], 0.0)
        ident = keep.tile([P, P], F32, name="ident")
        make_identity(nc, ident[:])

        g_rows = g.rearrange("(p q) t -> p q t", q=PACK)
        g_in = [keep.tile([P, T], F32, name=f"g_in{q}") for q in range(PACK)]
        sv_in = [keep.tile([P, T], F32, name=f"sv_in{a}") for a in range(BLOCKS)]
        x_in = [keep.tile([P, T], F32, name=f"x_in{a}", align_bytes=64) for a in range(BLOCKS)]
        wd_codes = keep.tile([P, 2 * R], U8, name="wd_codes", align_bytes=64)
        for q in range(PACK):
            nc.sync.dma_start(g_in[q][:], g_rows[:, q, :])
            if q == 0:
                nc.sync.dma_start(offsets[:], offs)
            nc.sync.dma_start(
                wd_plane[:].bitcast(I32)[32 * q : 32 * q + 4, :],
                wd_scales[0].bitcast(I32)[4 * q : 4 * q + 4, :],
            )

        def load_rows(tile, src, a):
            nc.sync.dma_start(tile[a][:], src[a * P : (a + 1) * P, :])

        nc.sync.dma_start(rw_rows[0:BLOCKS, :], rw.rearrange("o (b p) -> (o b) p", p=P))
        load_rows(sv_in, sv, 0)
        nc.sync.dma_start(wd_codes[:].bitcast(I32), wd_words[0].bitcast(I32))
        load_rows(sv_in, sv, 1)
        load_rows(sv_in, sv, 2)
        load_rows(sv_in, sv, 3)
        for a in range(BLOCKS):
            load_rows(x_in, xt, a)

        rw_turned = psum.tile([P, P], F32, name="rw_turned", tag="bank_b0")
        nc.tensor.transpose(rw_turned[:], rw_rows[:], ident[:])
        rw_col = keep.tile([P, BLOCKS], F32, name="rw_col", align_bytes=64)
        nc.scalar.copy(rw_col[:], rw_turned[:, 0:BLOCKS])

        g_picked = keep.tile([P, PACK, J], F32, name="g_picked")
        g_bf = [keep.tile([P, 2 * P, PACK], BF16, name=f"g_bf{h}", align_bytes=64) for h in range(2)]
        for q in range(PACK - 1):
            nc.vector.tensor_copy(g_picked[:, q, :], g_in[q][:].indirect(offsets[:]))
        for b in range(BLOCKS):
            cols = slice(b * P, (b + 1) * P)
            nc.vector.tensor_copy(
                g_picked[:, PACK - 1, cols],
                g_in[PACK - 1][:].indirect(offsets[:, b * P // 16 : (b + 1) * P // 16]),
            )
            nc.scalar.activation(
                g_bf[b // 2][:, (b % 2) * P : (b % 2 + 1) * P, :].rearrange("p (c i) q -> p c q i", i=4),
                g_picked[:, :, cols].rearrange("p q (c i) -> p c q i", i=4),
                COPY,
            )

        sv_picked = []

        def pick_sv(a):
            tag = "g_bf1" if a == 1 else f"sv_picked{a}"
            picked = keep.tile([P, J], F32, name=f"sv_picked{a}", tag=tag, align_bytes=64)
            nc.vector.tensor_copy(picked[:], sv_in[a][:].indirect(offsets[:]))
            sv_picked.append(picked)

        g_codes = [keep.tile([P, 2 * P], U32, name=f"g_codes{h}", align_bytes=64) for h in range(2)]
        g_plane = [keep.tile([P, 2 * P], U8, name=f"g_plane{h}", align_bytes=64) for h in range(2)]
        pick_sv(0)
        for h in range(2):
            nc.vector.quantize_mx(g_codes[h][:].bitcast(E5M2), g_plane[h][:], g_bf[h][:].rearrange("p j q -> p (j q)"))

        x_cast, x_picked = {}, {}

        def cast_x(a):
            x_cast[a] = keep.tile([P, T], BF16, name=f"x_cast{a}", align_bytes=64)
            nc.scalar.activation(x_cast[a][:], x_in[a][:], COPY)

        def pick_x(a):
            tag = {3: "x_bf0"}.get(a, f"x_picked{a}")
            x_picked[a] = keep.tile([P, J], BF16, name=f"x_picked{a}", tag=tag, align_bytes=64)
            if a in SCALAR_X:
                nc.scalar.activation(x_picked[a][:], x_cast[a][:].indirect(offsets[:]), COPY)
            else:
                nc.vector.tensor_copy(x_picked[a][:], x_in[a][:].indirect(offsets[:]))

        d_rw = keep.tile([P, BLOCKS, R], F32, name="d_rw")
        d_turned = [psum.tile([P, J], F32, name=f"d_turned{a}", tag=f"bank_b{a}") for a in range(BLOCKS)]
        for b in range(BLOCKS):
            cols = slice((b % 2) * P, (b % 2 + 1) * P)
            bank = psum.tile([P, R], F32, name=f"d{b}", tag=f"bank_a{b}")
            nc.tensor.matmul_mx(
                bank[:], lhsT=g_codes[b // 2][:, cols].bitcast(E5M2), lhsT_scale=g_plane[b // 2][:, cols],
                rhs=wd_codes[:].bitcast(E2M1), rhs_scale=wd_plane[:], start=True, stop=True,
            )
            nc.scalar.activation(d_rw[:, b, :], bank[:], COPY, scale=rw_col[:, b : b + 1])

        for b in range(BLOCKS):
            for a in range(BLOCKS):
                nc.tensor.transpose(d_turned[a][:, b * P : (b + 1) * P], d_rw[:, b, a * P : (a + 1) * P], ident[:])

        for a in range(1, BLOCKS):
            pick_sv(a)
        cast_x(0)
        pick_x(0)

        x_bf = [keep.tile([P, len(group) * P * PACK], BF16, name=f"x_bf{h}", align_bytes=64) for h, group in enumerate(X_GROUPS)]
        x_place = {a: (h, i) for h, group in enumerate(X_GROUPS) for i, a in enumerate(group)}
        dz_bf = keep.tile([P, R * PACK], BF16, name="dz_bf", align_bytes=64)

        def turn(rows, bank_tag, grouped, copy):
            words = rows[:].bitcast(F32)
            bank = psum.tile([P, 2, P], F32, name="turned", tag=bank_tag)
            for u in range(2):
                nc.tensor.transpose(bank[:, u, :], words[:, u::2], ident[:])
            copy(grouped.rearrange("p (c u) -> p c u", u=2), bank[:].rearrange("p u c -> p c u"))

        def turn_x(a, bank):
            h, i = x_place[a]
            turn(x_picked[a], f"bank_a{bank}", x_bf[h][:].bitcast(F32)[:, i * 2 * P : (i + 1) * 2 * P], nc.vector.tensor_copy if a == BLOCKS - 1 else nc.scalar.copy)

        dz_codes = keep.tile([P, R], U32, name="dz_codes", align_bytes=64)
        dz_plane = keep.tile([P, R], U8, name="dz_plane", align_bytes=64)
        x_codes = [keep.tile([P, len(group) * P], U32, name=f"x_codes{h}", align_bytes=64) for h, group in enumerate(X_GROUPS)]
        x_plane = [keep.tile([P, len(group) * P], U8, name=f"x_plane{h}", align_bytes=64) for h, group in enumerate(X_GROUPS)]

        def make_dz(a):
            rows = keep.tile([P, J], BF16, name=f"dz_rows{a}", align_bytes=64)
            nc.vector.scalar_tensor_tensor(rows[:], sv_picked[a][:], 0.0, d_turned[a][:], MAX, MULT)
            turn(rows, f"bank_a{(a + 2) % 4}", dz_bf[:].bitcast(F32)[:, a * 2 * P : (a + 1) * 2 * P], nc.scalar.copy)

        def quantise_x(h):
            nc.vector.quantize_mx(x_codes[h][:].bitcast(E4M3), x_plane[h][:], x_bf[h][:])

        def finish(a):
            h, i = x_place[a]
            cols = slice(i * P, (i + 1) * P)
            bank = psum.tile([P, R], F32, name=f"w{a}", tag=f"bank_b{a}")
            nc.tensor.matmul_mx(
                bank[:], lhsT=x_codes[h][:, cols].bitcast(E4M3), lhsT_scale=x_plane[h][:, cols],
                rhs=dz_codes[:].bitcast(E5M2), rhs_scale=dz_plane[:], start=True, stop=True,
            )
            result = keep.tile([P, R], F32, name=f"result{a}")
            if a < BLOCKS - 1:
                nc.scalar.activation(result[:], bank[:], COPY, scale=OUT_SCALE)
                nc.sync.dma_start(out[a * P : (a + 1) * P, :], result[:])
            else:
                for half in (slice(0, R // 2), slice(R // 2, R)):
                    nc.vector.tensor_scalar(result[:, half], bank[:, half], OUT_SCALE, None, MULT)
                    nc.sync.dma_start(out[a * P : (a + 1) * P, half], result[:, half])

        for a in range(BLOCKS):
            make_dz(a)
        turn_x(0, 2)
        pick_x(1)
        turn_x(1, 3)
        pick_x(2)
        turn_x(2, 0)
        nc.vector.quantize_mx(dz_codes[:].bitcast(E5M2), dz_plane[:], dz_bf[:])
        quantise_x(0)
        pick_x(3)
        finish(0)
        finish(1)
        turn_x(3, 1)
        quantise_x(1)
        finish(2)
        quantise_x(2)
        finish(3)
